import numpy as np
import ml_dtypes


def mxq(x, axis, fmt="e4m3"):
    dtype, down = {"e4m3": (ml_dtypes.float8_e4m3fn, 7), "e5m2": (ml_dtypes.float8_e5m2, 14)}[fmt]
    v = np.moveaxis(np.asarray(x, np.float32).astype(ml_dtypes.bfloat16).astype(np.float64), axis, -1)
    blocks = v.reshape(v.shape[:-1] + (-1, 32))
    amax = np.abs(blocks).max(-1, keepdims=True)
    byte = np.maximum(np.where(amax > 0, np.frexp(amax)[1] - 1 + 127, 0) - down, 1)
    scale = np.exp2(byte - 127.0)
    codes = (blocks / scale).astype(np.float32).astype(dtype).astype(np.float64)
    return np.moveaxis((codes * scale).reshape(v.shape), -1, axis)


WIDE = False


def mx_kscale(k):
    if not WIDE:
        return np.ones(k)
    levels = np.array([10, -10, 5, -5, 0])
    if k % 512:
        return np.exp2(np.random.permutation(np.resize(levels, k // 32))).repeat(32)
    a = np.empty((k // 512, 16))
    for p in range(k // 512):
        a[p, :8] = np.random.permutation(np.resize(levels, 8))
        for g in range(8):
            far = levels[np.abs(levels - a[p, g]) >= 10]
            a[p, g + 8] = far[np.random.randint(len(far))]
    return np.exp2(a.ravel()).repeat(32)


def f64(x):
    return np.asarray(x).astype(np.float64)


def striped(idx):
    return np.tile(idx.reshape(-1, 16).T, (8, 1)).astype(np.uint16)


def unstriped(offs):
    return offs[:16].T.reshape(-1).astype(np.int64)


E2M1 = np.array([0.0, 0.5, 1.0, 1.5, 2.0, 3.0, 4.0, 6.0, -0.0, -0.5, -1.0, -1.5, -2.0, -3.0, -4.0, -6.0])


def pack_weight(w, fmt):
    k, n = w.shape
    w = f64(np.asarray(w, np.float32).astype(ml_dtypes.bfloat16)).reshape(k // 32, 32, n)
    amax = np.abs(w).max(1)
    if fmt == "e4m3":
        byte = np.frexp(amax)[1] - 1 + 127 - 7
    else:
        mant, ex = np.frexp(amax / 6.0)
        byte = np.where(mant > 0.5, ex, ex - 1) + 127
    byte = np.clip(np.where(amax > 0, byte, 1), 1, 254)
    scaled = (w * np.exp2(127.0 - byte)[:, None, :]).reshape(k, n).astype(np.float32)
    by_word = np.ascontiguousarray(scaled.reshape(k // 512, 128, 4, n).transpose(0, 1, 3, 2))
    if fmt == "e4m3":
        words = by_word.astype(ml_dtypes.float8_e4m3fn).view(np.uint8)
    else:
        c = by_word.astype(ml_dtypes.float4_e2m1fn).view(np.uint8) & 0xF
        words = (c[..., 0::2] | (c[..., 1::2] << 4)).reshape(k // 512, 128, 2 * n)
    return np.ascontiguousarray(words), np.ascontiguousarray(byte.astype(np.uint8).reshape(k // 512, 16, n))


def unpack_weight(words, scales, fmt):
    g, _, n = scales.shape
    words = np.ascontiguousarray(words).reshape(g, 128, n, -1)
    if fmt == "e4m3":
        vals = words.view(ml_dtypes.float8_e4m3fn).astype(np.float64)
    else:
        nib = np.empty((g, 128, n, 4), np.uint8)
        nib[..., 0::2] = words & 0xF
        nib[..., 1::2] = words >> 4
        vals = E2M1[nib]
    vals = vals * np.repeat(np.exp2(scales.astype(np.float64) - 127.0), 8, axis=1)[..., None]
    return vals.transpose(0, 1, 3, 2).reshape(g * 512, n)


def gelu(v):
    return 0.5 * v * (1.0 + np.tanh(np.sqrt(2.0 / np.pi) * (v + 0.044715 * v**3)))


def striped8(idx):
    return np.concatenate([v.reshape(-1, 16).T for v in idx]).astype(np.uint16)


def unstriped8(offs):
    return np.stack([offs[16 * g:16 * g + 16].T.reshape(-1) for g in range(8)]).astype(np.int64)


def heads(h, wgt, idx8):
    r = np.arange(h.shape[0])
    return wgt[r // 4 % 128] * h[r[:, None], idx8[r % 512 // 64]]


K, T, S, T2, P, H, N = 1024, 4096, 1024, 2048, 1024, 1024, 512


def setup_inputs():
    n = np.random.standard_normal
    s = mx_kscale(K)[:, None]
    u = mx_kscale(H)[:, None]
    tab_words, tab_scales = pack_weight(n((K, T)) * s, "e4m3")
    w4_words, w4_scales = pack_weight(n((H, N)) / np.sqrt(H) / u, "e2m1")
    return {
        "tab_words": tab_words,
        "tab_scales": tab_scales,
        "offs": striped(np.random.permutation(T)[:S]),
        "w1": (0.38 * n((K, H)) / np.sqrt(K) / s).astype(np.float32),
        "b1": np.random.uniform(-1.0, 1.0, H).astype(np.float32),
        "gain": (1.5 * np.exp(0.3 * n(H)) * u[:, 0]).astype(np.float32),
        "page0": (n((H, T2)) * u).astype(np.float32),
        "wgs": np.exp(0.3 * n((128, S))).astype(np.float32),
        "offs2": striped(np.random.permutation(T2)[:S]),
        "wgt": np.repeat(np.random.uniform(0.5, 2.0, (8, P)), 16, axis=0).astype(np.float32),
        "offs3": striped8(np.stack([np.random.permutation(T2)[:P] for _ in range(8)])),
        "reach": np.random.uniform(0.2, 1.8, (H, P)).astype(np.float32),
        "w4_words": w4_words,
        "w4_scales": w4_scales,
        "b2": n(N).astype(np.float32),
    }


def reference(tab_words, tab_scales, offs, w1, b1, gain, page0, wgs, offs2, wgt, offs3, reach, w4_words, w4_scales, b2):
    v = unpack_weight(tab_words, tab_scales, "e4m3")[:, unstriped(offs)]
    w4 = unpack_weight(w4_words, w4_scales, "e2m1")
    arg = (mxq(f64(w1), 0, "e4m3").T @ v) + f64(b1)[:, None]
    h = f64(gain)[:, None] * np.sin(arg)
    page = f64(page0).copy()
    page[:, unstriped(offs2)] = np.tile(f64(wgs), (H // 128, 1)) * h
    x = heads(page, f64(wgt), unstriped8(offs3))
    z = mxq(x * f64(reach), 0, "e4m3")
    return (w4.T @ z) + f64(b2)[:, None]

@@ -1,0 +1,309 @@
+import math
+from contextlib import ExitStack
+
+import concourse.mybir as mybir
+from concourse.masks import make_identity
+
+K, T, S, T2, M, H, N = 1024, 4096, 1024, 2048, 1024, 1024, 512
+FLOPS = 2 * K * H * S + 2 * H * N * M
+
+F32 = mybir.dt.float32
+BF16 = mybir.dt.bfloat16
+I32 = mybir.dt.int32
+U32 = mybir.dt.uint32
+U16 = mybir.dt.uint16
+U8 = mybir.dt.uint8
+FP8X4 = mybir.dt.float8_e4m3fn_x4
+FP4X4 = mybir.dt.float4_e2m1fn_x4
+ALU = mybir.AluOpType
+ACT = mybir.ActivationFunctionType
+
+P = 128
+PACK = 4
+PASS = P * PACK
+BANK = 512
+GROUP = 16
+FIRST_CUTS = (256, 256, 512)
+LAST_CUTS = (256, 256, 256, 128, 128)
+
+
+def spans(widths):
+    start = 0
+    result = []
+    for width in widths:
+        result.append((start, start + width))
+        start = start + width
+    return result
+
+
+def tile_list_suction_grasp_scores_kernel(
+    tc, tab_words, tab_scales, offs, w1, b1, gain, page0, wgs, offs2, wgt, offs3, reach, w4_words, w4_scales, b2, out
+):
+    nc = tc.nc
+    with ExitStack() as ctx:
+        keep = ctx.enter_context(tc.tile_pool(name="keep", bufs=1))
+        ring = ctx.enter_context(tc.tile_pool(name="ring", bufs=1))
+        psum = ctx.enter_context(tc.psum_pool(name="psum", bufs=1))
+
+        list1 = keep.tile([P, S // 16], U16, name="list1")
+        list2 = keep.tile([P, S // 16], U16, name="list2")
+        list3 = keep.tile([P, M // 16], U16, name="list3")
+
+        tab_planes = keep.tile([P, T], U8, name="tab_planes", align_bytes=64)
+        w4_planes = keep.tile([P, 2, N], U8, name="w4_planes", align_bytes=64)
+        w4_codes = keep.tile([P, 2, 2 * N], U8, name="w4_codes", align_bytes=64)
+        b1_t = keep.tile([P, 2, PACK], F32, name="b1_t")
+        gain_t = keep.tile([P, 2, PACK], F32, name="gain_t")
+        b2_t = keep.tile([P, N // P], F32, name="b2_t")
+        ident = keep.tile([P, P], F32, name="ident")
+
+        nc.vector.memset(tab_planes[:].bitcast(I32), 0)
+        nc.vector.memset(w4_planes[:].rearrange("p a n -> p (a n)").bitcast(I32), 0)
+        nc.gpsimd.dma_start(b1_t[:], b1.rearrange("(b p i) -> p b i", b=2, i=PACK))
+        nc.gpsimd.dma_start(gain_t[:], gain.rearrange("(b p i) -> p b i", b=2, i=PACK))
+        for q in range(4):
+            nc.gpsimd.dma_start(
+                w4_planes[32 * q : 32 * q + 4, :, :].bitcast(I32),
+                w4_scales[:, 4 * q : 4 * q + 4, :].rearrange("a r n -> r a n").bitcast(I32),
+            )
+        with nc.allow_non_contiguous_dma(reason="one bias value a partition"):
+            nc.gpsimd.dma_start(b2_t[:], b2.rearrange("(t p) -> p t", p=P))
+        make_identity(nc, ident[:])
+
+        def load_w1(b, a):
+            raw = ring.tile([P, PACK, PASS], F32, name="w1_raw", tag="w1_raw", bufs=2)
+            rows = w1[a * PASS : (a + 1) * PASS, b * PASS : (b + 1) * PASS]
+            nc.sync.dma_start(raw[:], rows.rearrange("(p j) c -> p j c", j=PACK))
+            return raw
+
+        def load_page(b, i):
+            page = keep.tile([P, T2], F32, name="page_%d_%d" % (b, i))
+            rows = page0[b * PASS : (b + 1) * PASS, :].rearrange("(p i) c -> p i c", i=PACK)
+            nc.sync.dma_start(page[:], rows[:, i, :])
+            return page
+
+        def load_reach(b):
+            factor = keep.tile([P, PACK, M], F32, name="factor_%d" % b)
+            nc.sync.dma_start(factor[:], reach[b * PASS : (b + 1) * PASS, :].rearrange("(p i) m -> p i m", i=PACK))
+            return factor
+
+        wgs_rows = wgs.rearrange("(p i) s -> p i s", i=PACK)
+        wgs_first = keep.tile([P, S], F32, name="wgs_first")
+        wgs_rest = keep.tile([P, PACK - 1, S], F32, name="wgs_rest")
+        wgt_t = keep.tile([P, M], F32, name="wgt_t")
+
+        nc.sync.dma_start(list1[:], offs)
+        w1_raw = {(0, 0): load_w1(0, 0)}
+        for q in range(4):
+            nc.sync.dma_start(
+                tab_planes[32 * q : 32 * q + 8, :].bitcast(I32), tab_scales[:, 4 * q : 4 * q + 4, :].bitcast(I32)
+            )
+        w1_raw[0, 1] = load_w1(0, 1)
+        tab = []
+        for a in range(2):
+            words = ring.tile([P, T], U32, name="tab_words_t", tag="wide", bufs=2, align_bytes=64)
+            nc.sync.dma_start(words[:].bitcast(I32), tab_words[a].rearrange("p t i -> p (t i)").bitcast(I32))
+            tab.append(words)
+        nc.sync.dma_start(list2[:], offs2)
+        pages = {(0, 0): load_page(0, 0)}
+        for q in range(4):
+            nc.sync.dma_start(wgs_first[32 * q : 32 * (q + 1), :], wgs_rows[:, 0, :])
+        pages[0, 1] = load_page(0, 1)
+        for q in range(4):
+            nc.sync.dma_start(wgs_rest[32 * q : 32 * (q + 1), :, :], wgs_rows[:, 1:PACK, :])
+        pages[0, 2] = load_page(0, 2)
+        for a in range(2):
+            w1_raw[1, a] = load_w1(1, a)
+        pages[0, 3] = load_page(0, 3)
+        nc.sync.dma_start(wgt_t[:], wgt)
+        nc.sync.dma_start(list3[:], offs3)
+        factors = [load_reach(0)]
+        pages[1, 0] = load_page(1, 0)
+        factors.append(load_reach(1))
+        for i in range(1, PACK):
+            pages[1, i] = load_page(1, i)
+        nc.sync.dma_start(w4_codes[:].bitcast(I32), w4_words.rearrange("a p n -> p a n").bitcast(I32))
+
+        half_bias = keep.tile([P, 2, PACK], F32, name="half_bias")
+        minus_two_gain = keep.tile([P, 2, PACK], F32, name="minus_two_gain")
+        nc.vector.tensor_scalar(half_bias[:], b1_t[:], 0.5, -math.pi / 4, ALU.mult, ALU.add)
+        nc.vector.tensor_scalar(minus_two_gain[:], gain_t[:], -2.0, None, ALU.mult)
+
+        w1_codes = {}
+        w1_planes = {}
+
+        def quantise_w1(b, a, copy):
+            grouped = ring.tile([P, PACK, P, PACK], BF16, name="grouped", tag="bf", bufs=3, align_bytes=64)
+            copy(
+                grouped[:].rearrange("p t m j -> p m j t"),
+                w1_raw[b, a][:].rearrange("p j (m t) -> p m j t", t=PACK),
+            )
+            codes = keep.tile([P, PASS], U32, name="w1_codes_%d_%d" % (b, a), align_bytes=64)
+            plane = keep.tile([P, PASS], U8, name="w1_plane_%d_%d" % (b, a), align_bytes=64)
+            nc.vector.quantize_mx(
+                out=codes[:].bitcast(FP8X4), scales=plane[:], in_=grouped[:].rearrange("p t m j -> p (t m j)")
+            )
+            w1_codes[b, a] = codes
+            w1_planes[b, a] = plane
+
+        for a in range(2):
+            quantise_w1(0, a, nc.vector.tensor_copy)
+
+        v_planes = keep.tile([P, S], U8, name="v_planes", align_bytes=64)
+        v_words = [keep.tile([P, S], U32, name="v_words_%d" % a, align_bytes=64) for a in range(2)]
+        nc.vector.tensor_copy(v_planes[:], tab_planes[:].indirect(list1[:]))
+        nc.vector.tensor_copy(v_words[0][:], tab[0][:].indirect(list1[:]))
+        for lo, hi in spans(FIRST_CUTS):
+            nc.vector.tensor_copy(v_words[1][:, lo:hi], tab[1][:].indirect(list1[:, lo // 16 : hi // 16]))
+
+        def first_stage(b, i, matmul_cuts, tail_cuts):
+            h = ring.tile([P, S], F32, name="h", tag="h", bufs=3)
+            rows = slice(i * P, (i + 1) * P)
+            done = 0
+            todo = spans(tail_cuts)
+            for lo, hi in spans(matmul_cuts):
+                acc = psum.tile([P, hi - lo], F32, name="acc", tag="mm", bufs=4)
+                for a in range(2):
+                    nc.tensor.matmul_mx(
+                        out=acc[:],
+                        lhsT=w1_codes[b, a][:, rows].bitcast(FP8X4),
+                        lhsT_scale=w1_planes[b, a][:, rows],
+                        rhs=v_words[a][:, lo:hi].bitcast(FP8X4),
+                        rhs_scale=v_planes[PACK * a :, lo:hi],
+                        start=(a == 0),
+                        stop=(a == 1),
+                    )
+                nc.scalar.activation(h[:, lo:hi], acc[:], ACT.Sin, bias=half_bias[:, b, i : i + 1], scale=0.5)
+                if hi == todo[done][1]:
+                    s0, s1 = todo[done]
+                    done = done + 1
+                    nc.scalar.activation(h[:, s0:s1], h[:, s0:s1], ACT.Square)
+                    nc.scalar.activation(
+                        h[:, s0:s1],
+                        h[:, s0:s1],
+                        ACT.Identity,
+                        bias=gain_t[:, b, i : i + 1],
+                        scale=minus_two_gain[:, b, i : i + 1],
+                    )
+                    weights = wgs_first[:, s0:s1] if i == 0 else wgs_rest[:, i - 1, s0:s1]
+                    nc.vector.tensor_tensor(
+                        pages[b, i][:].indirect(list2[:, s0 // 16 : s1 // 16]), h[:, s0:s1], weights, ALU.mult
+                    )
+
+        wgt_cols = keep.tile([P, M // P, P // GROUP], F32, name="wgt_cols")
+
+        def turn_wgt():
+            for half in range(2):
+                bank = psum.tile([P, PACK, P], F32, name="turned", tag="fw", bufs=2)
+                for u in range(PACK):
+                    mb = half * PACK + u
+                    nc.tensor.transpose(bank[:, u, :], wgt_t[:, mb * P : (mb + 1) * P], ident[:])
+                nc.scalar.copy(wgt_cols[:, half * PACK : (half + 1) * PACK, :], bank[:, :, 0:P:GROUP])
+
+        def weigh_reach(b, mb):
+            cols = slice(mb * P, (mb + 1) * P)
+            turned = psum.tile([P, PACK, P], F32, name="turned", tag="fw", bufs=2)
+            for i in range(PACK):
+                nc.tensor.transpose(turned[:, i, :], factors[b][:, i, cols], ident[:])
+            scaled = ring.tile([P, PACK, P], F32, name="scaled", tag="scaled", bufs=3)
+            for g in range(P // GROUP):
+                run = slice(g * GROUP, (g + 1) * GROUP)
+                nc.scalar.activation(scaled[:, :, run], turned[:, :, run], ACT.Copy, scale=wgt_cols[:, mb, g : g + 1])
+            back = psum.tile([P, PACK, P], F32, name="back", tag="bk", bufs=2)
+            for i in range(PACK):
+                nc.tensor.transpose(back[:, i, :], scaled[:, i, :], ident[:])
+            nc.scalar.copy(factors[b][:, :, cols], back[:])
+
+        z_codes = [keep.tile([P, M], U32, name="z_codes_%d" % b, align_bytes=64) for b in range(2)]
+        z_planes = [keep.tile([P, M], U8, name="z_planes_%d" % b, align_bytes=64) for b in range(2)]
+
+        def collect(b, picked, lo, hi):
+            for i in range(PACK):
+                nc.vector.tensor_tensor(
+                    picked[:, i, lo:hi],
+                    pages[b, i][:].indirect(list3[:, lo // 16 : hi // 16]),
+                    factors[b][:, i, lo:hi],
+                    ALU.mult,
+                )
+
+        def quantise_z(b, picked, lo, hi, copy):
+            z = ring.tile([P, hi - lo, PACK], BF16, name="z", tag="bf", bufs=3, align_bytes=64)
+            copy(
+                z[:].rearrange("p (c k) i -> p c i k", k=4),
+                picked[:, :, lo:hi].rearrange("p i (c k) -> p c i k", k=4),
+            )
+            nc.vector.quantize_mx(
+                out=z_codes[b][:, lo:hi].bitcast(FP8X4),
+                scales=z_planes[b][:, lo:hi],
+                in_=z[:].rearrange("p m i -> p (m i)"),
+            )
+
+        def second_pass(b, bank, slot, nt, lo, hi, start, stop):
+            nc.tensor.matmul_mx(
+                out=bank[:, slot, :],
+                lhsT=w4_codes[:, b, 2 * nt * P : 2 * (nt + 1) * P].bitcast(FP4X4),
+                lhsT_scale=w4_planes[:, b, nt * P : (nt + 1) * P],
+                rhs=z_codes[b][:, lo:hi].bitcast(FP8X4),
+                rhs_scale=z_planes[b][:, lo:hi],
+                start=start,
+                stop=stop,
+            )
+
+        whole = (BANK, BANK)
+        first_stage(0, 0, FIRST_CUTS, FIRST_CUTS)
+        for i in range(1, PACK):
+            first_stage(0, i, whole, (S,))
+        for a in range(2):
+            quantise_w1(1, a, nc.scalar.copy)
+        first_stage(1, 0, whole, (S,))
+        turn_wgt()
+        for mb in range(M // P):
+            weigh_reach(0, mb)
+        picked0 = ring.tile([P, PACK, M], F32, name="picked", tag="wide", bufs=2, align_bytes=64)
+        collect(0, picked0, 0, M)
+        for i in range(1, PACK):
+            first_stage(1, i, whole, (S,))
+        for mb in range(M // P):
+            weigh_reach(1, mb)
+        for lo, hi in spans(whole):
+            quantise_z(0, picked0, lo, hi, nc.scalar.copy)
+
+        tags = [("mm", 4)] * 4 + [("fw", 2)] * 2 + [("bk", 2)] * 2
+        banks = []
+        used = 0
+        for lo, hi in spans(LAST_CUTS):
+            per_bank = BANK // (hi - lo)
+            mine = []
+            for first in range(0, N // P, per_bank):
+                tag, bufs = tags[used]
+                used = used + 1
+                bank = psum.tile([P, per_bank, hi - lo], F32, name="scores", tag=tag, bufs=bufs)
+                for slot in range(per_bank):
+                    second_pass(0, bank, slot, first + slot, lo, hi, slot == 0, False)
+                mine.append((bank, first, per_bank))
+            banks.append(mine)
+
+        picked1 = ring.tile([P, PACK, M], F32, name="picked", tag="wide", bufs=2, align_bytes=64)
+        out_rows = out.rearrange("(t p) m -> p t m", p=P)
+        last = len(LAST_CUTS) - 1
+        for c, (lo, hi) in enumerate(spans(LAST_CUTS)):
+            collect(1, picked1, lo, hi)
+            quantise_z(1, picked1, lo, hi, nc.vector.tensor_copy if c == last else nc.scalar.copy)
+            staged = ring.tile([P, N // P, hi - lo], F32, name="staged", tag="h", bufs=3)
+            for bank, first, per_bank in banks[c]:
+                for slot in range(per_bank):
+                    second_pass(1, bank, slot, first + slot, lo, hi, False, slot == per_bank - 1)
+                if c == last:
+                    nc.vector.tensor_tensor(
+                        staged[:, first : first + per_bank, :],
+                        bank[:],
+                        b2_t[:, first : first + per_bank].unsqueeze(2).to_broadcast([P, per_bank, hi - lo]),
+                        ALU.add,
+                    )
+                else:
+                    for slot in range(per_bank):
+                        nt = first + slot
+                        nc.scalar.activation(
+                            staged[:, nt, :], bank[:, slot, :], ACT.Identity, bias=b2_t[:, nt : nt + 1]
+                        )
+            nc.sync.dma_start(out_rows[:, :, lo:hi], staged[:])

@@ -23,8 +23,9 @@ PACK = 4
 PASS = P * PACK
 BANK = 512
 GROUP = 16
+RUNS = 8
 FIRST_CUTS = (256, 256, 512)
-LAST_CUTS = (256, 256, 256, 128, 128)
+LAST_CUTS = (512, 256, 128, 128)
 
 
 def spans(widths):
@@ -49,7 +50,7 @@ def tile_list_suction_grasp_scores_kernel(
         list2 = keep.tile([P, S // 16], U16, name="list2")
         list3 = keep.tile([P, M // 16], U16, name="list3")
 
-        tab_planes = keep.tile([P, T], U8, name="tab_planes", align_bytes=64)
+        tab_planes = ring.tile([P, T], U8, name="tab_planes", tag="planes", align_bytes=64)
         w4_planes = keep.tile([P, 2, N], U8, name="w4_planes", align_bytes=64)
         w4_codes = keep.tile([P, 2, 2 * N], U8, name="w4_codes", align_bytes=64)
         b1_t = keep.tile([P, 2, PACK], F32, name="b1_t")
@@ -57,21 +58,19 @@ def tile_list_suction_grasp_scores_kernel(
         b2_t = keep.tile([P, N // P], F32, name="b2_t")
         ident = keep.tile([P, P], F32, name="ident")
 
+        v_planes = keep.tile([P, S], U8, name="v_planes", align_bytes=64)
         nc.vector.memset(tab_planes[:].bitcast(I32), 0)
-        nc.vector.memset(w4_planes[:].rearrange("p a n -> p (a n)").bitcast(I32), 0)
-        nc.gpsimd.dma_start(b1_t[:], b1.rearrange("(b p i) -> p b i", b=2, i=PACK))
-        nc.gpsimd.dma_start(gain_t[:], gain.rearrange("(b p i) -> p b i", b=2, i=PACK))
         for q in range(4):
             nc.gpsimd.dma_start(
-                w4_planes[32 * q : 32 * q + 4, :, :].bitcast(I32),
-                w4_scales[:, 4 * q : 4 * q + 4, :].rearrange("a r n -> r a n").bitcast(I32),
+                tab_planes[32 * q : 32 * q + 8, :].bitcast(I32), tab_scales[:, 4 * q : 4 * q + 4, :].bitcast(I32)
             )
-        with nc.allow_non_contiguous_dma(reason="one bias value a partition"):
-            nc.gpsimd.dma_start(b2_t[:], b2.rearrange("(t p) -> p t", p=P))
+        nc.vector.memset(w4_planes[:].rearrange("p a n -> p (a n)").bitcast(I32), 0)
+        nc.scalar.dma_start(b1_t[:], b1.rearrange("(b p i) -> p b i", b=2, i=PACK))
+        nc.scalar.dma_start(gain_t[:], gain.rearrange("(b p i) -> p b i", b=2, i=PACK))
         make_identity(nc, ident[:])
 
         def load_w1(b, a):
-            raw = ring.tile([P, PACK, PASS], F32, name="w1_raw", tag="w1_raw", bufs=2)
+            raw = ring.tile([P, PACK, PASS], F32, name="w1_raw", tag="raw%d" % a)
             rows = w1[a * PASS : (a + 1) * PASS, b * PASS : (b + 1) * PASS]
             nc.sync.dma_start(raw[:], rows.rearrange("(p j) c -> p j c", j=PACK))
             return raw
@@ -82,66 +81,84 @@ def tile_list_suction_grasp_scores_kernel(
             nc.sync.dma_start(page[:], rows[:, i, :])
             return page
 
-        def load_reach(b):
-            factor = keep.tile([P, PACK, M], F32, name="factor_%d" % b)
-            nc.sync.dma_start(factor[:], reach[b * PASS : (b + 1) * PASS, :].rearrange("(p i) m -> p i m", i=PACK))
-            return factor
+        factor = keep.tile([P, RUNS, M], F32, name="factor")
+        reach_runs = reach.rearrange("(b g r) m -> g r b m", b=2, g=RUNS)
 
         wgs_rows = wgs.rearrange("(p i) s -> p i s", i=PACK)
-        wgs_first = keep.tile([P, S], F32, name="wgs_first")
-        wgs_rest = keep.tile([P, PACK - 1, S], F32, name="wgs_rest")
+        wgs_t = {}
+
+        def load_wgs(i, pool, tag):
+            wgs_t[i] = pool.tile([P, S], F32, name="wgs_%d" % i, tag=tag)
+            for q in range(4):
+                nc.sync.dma_start(wgs_t[i][32 * q : 32 * (q + 1), :], wgs_rows[:, i, :])
+
         wgt_t = keep.tile([P, M], F32, name="wgt_t")
 
         nc.sync.dma_start(list1[:], offs)
-        w1_raw = {(0, 0): load_w1(0, 0)}
-        for q in range(4):
-            nc.sync.dma_start(
-                tab_planes[32 * q : 32 * q + 8, :].bitcast(I32), tab_scales[:, 4 * q : 4 * q + 4, :].bitcast(I32)
-            )
-        w1_raw[0, 1] = load_w1(0, 1)
+        w1_raw = {(0, a): load_w1(0, a) for a in range(2)}
         tab = []
         for a in range(2):
-            words = ring.tile([P, T], U32, name="tab_words_t", tag="wide", bufs=2, align_bytes=64)
+            words = ring.tile([P, T], U32, name="tab_words_t", tag="wide%d" % a, align_bytes=64)
             nc.sync.dma_start(words[:].bitcast(I32), tab_words[a].rearrange("p t i -> p (t i)").bitcast(I32))
             tab.append(words)
         nc.sync.dma_start(list2[:], offs2)
         pages = {(0, 0): load_page(0, 0)}
-        for q in range(4):
-            nc.sync.dma_start(wgs_first[32 * q : 32 * (q + 1), :], wgs_rows[:, 0, :])
+        load_wgs(0, keep, "wgs0")
         pages[0, 1] = load_page(0, 1)
-        for q in range(4):
-            nc.sync.dma_start(wgs_rest[32 * q : 32 * (q + 1), :, :], wgs_rows[:, 1:PACK, :])
-        pages[0, 2] = load_page(0, 2)
+        load_wgs(1, keep, "wgs1")
         for a in range(2):
             w1_raw[1, a] = load_w1(1, a)
+        pages[0, 2] = load_page(0, 2)
+        load_wgs(2, keep, "wgs2")
+        load_wgs(3, keep, "wgs3")
         pages[0, 3] = load_page(0, 3)
-        nc.sync.dma_start(wgt_t[:], wgt)
-        nc.sync.dma_start(list3[:], offs3)
-        factors = [load_reach(0)]
-        pages[1, 0] = load_page(1, 0)
-        factors.append(load_reach(1))
-        for i in range(1, PACK):
+        for i in range(PACK):
             pages[1, i] = load_page(1, i)
+        nc.sync.dma_start(wgt_t[:], wgt)
+        for g in range(RUNS):
+            nc.sync.dma_start(factor[:, g, :], reach_runs[g])
+        nc.sync.dma_start(list3[:], offs3)
         nc.sync.dma_start(w4_codes[:].bitcast(I32), w4_words.rearrange("a p n -> p a n").bitcast(I32))
+        for q in range(4):
+            nc.sync.dma_start(
+                w4_planes[32 * q : 32 * q + 4, :, :].bitcast(I32),
+                w4_scales[:, 4 * q : 4 * q + 4, :].rearrange("a r n -> r a n").bitcast(I32),
+            )
+        with nc.allow_non_contiguous_dma(reason="one bias value a partition"):
+            nc.sync.dma_start(b2_t[:], b2.rearrange("(t p) -> p t", p=P))
+
+        psum_banks = [psum.tile([P, BANK], F32, name="bank%d" % k) for k in range(8)]
+        h_tiles = [keep.tile([P, S], F32, name="h%d" % k) for k in range(3)]
+        bf_tiles = [keep.tile([P, 2048], BF16, name="bf%d" % k, align_bytes=64) for k in range(2)]
+        scaled_tiles = [keep.tile([P, 2, PACK, P], F32, name="scaled%d" % k) for k in range(2)]
+        turns = {"bank": 0, "h": 0, "bf": 0, "scaled": 0}
+
+        def take(kind, tiles):
+            tile = tiles[turns[kind] % len(tiles)]
+            turns[kind] = turns[kind] + 1
+            return tile
+
+        def take_bank(count, width):
+            return take("bank", psum_banks)[:, 0 : count * width].rearrange("p (u w) -> p u w", u=count)
 
         half_bias = keep.tile([P, 2, PACK], F32, name="half_bias")
         minus_two_gain = keep.tile([P, 2, PACK], F32, name="minus_two_gain")
-        nc.vector.tensor_scalar(half_bias[:], b1_t[:], 0.5, -math.pi / 4, ALU.mult, ALU.add)
-        nc.vector.tensor_scalar(minus_two_gain[:], gain_t[:], -2.0, None, ALU.mult)
+        nc.gpsimd.tensor_scalar(half_bias[:], b1_t[:], 0.5, -math.pi / 4, ALU.mult, ALU.add)
+        nc.scalar.activation(minus_two_gain[:], gain_t[:], ACT.Copy, scale=-2.0)
 
         w1_codes = {}
         w1_planes = {}
 
         def quantise_w1(b, a, copy):
-            grouped = ring.tile([P, PACK, P, PACK], BF16, name="grouped", tag="bf", bufs=3, align_bytes=64)
+            grouped = take("bf", bf_tiles)
             copy(
-                grouped[:].rearrange("p t m j -> p m j t"),
+                grouped[:].rearrange("p (t m j) -> p m j t", t=PACK, j=PACK),
                 w1_raw[b, a][:].rearrange("p j (m t) -> p m j t", t=PACK),
             )
             codes = keep.tile([P, PASS], U32, name="w1_codes_%d_%d" % (b, a), align_bytes=64)
             plane = keep.tile([P, PASS], U8, name="w1_plane_%d_%d" % (b, a), align_bytes=64)
             nc.vector.quantize_mx(
-                out=codes[:].bitcast(FP8X4), scales=plane[:], in_=grouped[:].rearrange("p t m j -> p (t m j)")
+                out=codes[:].bitcast(FP8X4), scales=plane[:], in_=grouped[:]
             )
             w1_codes[b, a] = codes
             w1_planes[b, a] = plane
@@ -149,23 +166,25 @@ def tile_list_suction_grasp_scores_kernel(
         for a in range(2):
             quantise_w1(0, a, nc.vector.tensor_copy)
 
-        v_planes = keep.tile([P, S], U8, name="v_planes", align_bytes=64)
-        v_words = [keep.tile([P, S], U32, name="v_words_%d" % a, align_bytes=64) for a in range(2)]
         nc.vector.tensor_copy(v_planes[:], tab_planes[:].indirect(list1[:]))
+        v_words = [
+            keep.tile([P, S], U32, name="v_words_0", align_bytes=64),
+            ring.tile([P, S], U32, name="v_words_1", tag="planes", align_bytes=64),
+        ]
         nc.vector.tensor_copy(v_words[0][:], tab[0][:].indirect(list1[:]))
         for lo, hi in spans(FIRST_CUTS):
             nc.vector.tensor_copy(v_words[1][:, lo:hi], tab[1][:].indirect(list1[:, lo // 16 : hi // 16]))
 
         def first_stage(b, i, matmul_cuts, tail_cuts):
-            h = ring.tile([P, S], F32, name="h", tag="h", bufs=3)
+            h = take("h", h_tiles)
             rows = slice(i * P, (i + 1) * P)
             done = 0
             todo = spans(tail_cuts)
             for lo, hi in spans(matmul_cuts):
-                acc = psum.tile([P, hi - lo], F32, name="acc", tag="mm", bufs=4)
+                acc = take("bank", psum_banks)[:, 0 : hi - lo]
                 for a in range(2):
                     nc.tensor.matmul_mx(
-                        out=acc[:],
+                        out=acc,
                         lhsT=w1_codes[b, a][:, rows].bitcast(FP8X4),
                         lhsT_scale=w1_planes[b, a][:, rows],
                         rhs=v_words[a][:, lo:hi].bitcast(FP8X4),
@@ -173,7 +192,7 @@ def tile_list_suction_grasp_scores_kernel(
                         start=(a == 0),
                         stop=(a == 1),
                     )
-                nc.scalar.activation(h[:, lo:hi], acc[:], ACT.Sin, bias=half_bias[:, b, i : i + 1], scale=0.5)
+                nc.scalar.activation(h[:, lo:hi], acc, ACT.Sin, bias=half_bias[:, b, i : i + 1], scale=0.5)
                 if hi == todo[done][1]:
                     s0, s1 = todo[done]
                     done = done + 1
@@ -185,7 +204,7 @@ def tile_list_suction_grasp_scores_kernel(
                         bias=gain_t[:, b, i : i + 1],
                         scale=minus_two_gain[:, b, i : i + 1],
                     )
-                    weights = wgs_first[:, s0:s1] if i == 0 else wgs_rest[:, i - 1, s0:s1]
+                    weights = wgs_t[i][:, s0:s1]
                     nc.vector.tensor_tensor(
                         pages[b, i][:].indirect(list2[:, s0 // 16 : s1 // 16]), h[:, s0:s1], weights, ALU.mult
                     )
@@ -194,56 +213,61 @@ def tile_list_suction_grasp_scores_kernel(
 
         def turn_wgt():
             for half in range(2):
-                bank = psum.tile([P, PACK, P], F32, name="turned", tag="fw", bufs=2)
+                bank = take_bank(PACK, P)
                 for u in range(PACK):
                     mb = half * PACK + u
                     nc.tensor.transpose(bank[:, u, :], wgt_t[:, mb * P : (mb + 1) * P], ident[:])
                 nc.scalar.copy(wgt_cols[:, half * PACK : (half + 1) * PACK, :], bank[:, :, 0:P:GROUP])
 
-        def weigh_reach(b, mb):
+        def weigh_reach(mb):
             cols = slice(mb * P, (mb + 1) * P)
-            turned = psum.tile([P, PACK, P], F32, name="turned", tag="fw", bufs=2)
-            for i in range(PACK):
-                nc.tensor.transpose(turned[:, i, :], factors[b][:, i, cols], ident[:])
-            scaled = ring.tile([P, PACK, P], F32, name="scaled", tag="scaled", bufs=3)
-            for g in range(P // GROUP):
-                run = slice(g * GROUP, (g + 1) * GROUP)
-                nc.scalar.activation(scaled[:, :, run], turned[:, :, run], ACT.Copy, scale=wgt_cols[:, mb, g : g + 1])
-            back = psum.tile([P, PACK, P], F32, name="back", tag="bk", bufs=2)
-            for i in range(PACK):
-                nc.tensor.transpose(back[:, i, :], scaled[:, i, :], ident[:])
-            nc.scalar.copy(factors[b][:, :, cols], back[:])
+            scaled = take("scaled", scaled_tiles)
+            for half in range(2):
+                turned = take_bank(PACK, P)
+                for u in range(PACK):
+                    nc.tensor.transpose(turned[:, u, :], factor[:, half * PACK + u, cols], ident[:])
+                for u in range(PACK):
+                    g = half * PACK + u
+                    nc.scalar.activation(
+                        scaled[:, :, :, g * GROUP : (g + 1) * GROUP],
+                        turned[:, u, :].rearrange("m (p i b) -> m b i p", i=PACK, b=2),
+                        ACT.Copy,
+                        scale=wgt_cols[:, mb, g : g + 1],
+                    )
+            for b in range(2):
+                back = take_bank(PACK, P)
+                for i in range(PACK):
+                    nc.tensor.transpose(back[:, i, :], scaled[:, b, i, :], ident[:])
+                nc.scalar.copy(factor[:, b * PACK : (b + 1) * PACK, cols], back)
 
-        z_codes = [keep.tile([P, M], U32, name="z_codes_%d" % b, align_bytes=64) for b in range(2)]
         z_planes = [keep.tile([P, M], U8, name="z_planes_%d" % b, align_bytes=64) for b in range(2)]
 
         def collect(b, picked, lo, hi):
             for i in range(PACK):
                 nc.vector.tensor_tensor(
-                    picked[:, i, lo:hi],
+                    picked[:, i, :],
                     pages[b, i][:].indirect(list3[:, lo // 16 : hi // 16]),
-                    factors[b][:, i, lo:hi],
+                    factor[:, b * PACK + i, lo:hi],
                     ALU.mult,
                 )
 
-        def quantise_z(b, picked, lo, hi, copy):
-            z = ring.tile([P, hi - lo, PACK], BF16, name="z", tag="bf", bufs=3, align_bytes=64)
+        def quantise_z(b, picked, lo, hi, copy, z, codes):
             copy(
-                z[:].rearrange("p (c k) i -> p c i k", k=4),
-                picked[:, :, lo:hi].rearrange("p i (c k) -> p c i k", k=4),
+                z.rearrange("p (c k i) -> p c i k", k=4, i=PACK),
+                picked.rearrange("p i (c k) -> p c i k", k=4),
             )
             nc.vector.quantize_mx(
-                out=z_codes[b][:, lo:hi].bitcast(FP8X4),
+                out=codes.bitcast(FP8X4),
                 scales=z_planes[b][:, lo:hi],
-                in_=z[:].rearrange("p m i -> p (m i)"),
+                in_=z,
             )
 
-        def second_pass(b, bank, slot, nt, lo, hi, start, stop):
+        def second_pass(b, codes, bank, slot, nt, lo, hi, start, stop):
             nc.tensor.matmul_mx(
                 out=bank[:, slot, :],
                 lhsT=w4_codes[:, b, 2 * nt * P : 2 * (nt + 1) * P].bitcast(FP4X4),
                 lhsT_scale=w4_planes[:, b, nt * P : (nt + 1) * P],
-                rhs=z_codes[b][:, lo:hi].bitcast(FP8X4),
+                rhs=codes.bitcast(FP8X4),
                 rhs_scale=z_planes[b][:, lo:hi],
                 start=start,
                 stop=stop,
@@ -251,52 +275,53 @@ def tile_list_suction_grasp_scores_kernel(
 
         whole = (BANK, BANK)
         first_stage(0, 0, FIRST_CUTS, FIRST_CUTS)
-        for i in range(1, PACK):
+        for i in range(1, PACK - 1):
             first_stage(0, i, whole, (S,))
         for a in range(2):
             quantise_w1(1, a, nc.scalar.copy)
-        first_stage(1, 0, whole, (S,))
+        for a in (1, 0):
+            h_tiles.append(ring.tile([P, S], F32, name="h_late%d" % a, tag="raw%d" % a))
+        first_stage(0, PACK - 1, whole, (S,))
+        for i in range(PACK):
+            first_stage(1, i, whole, (S,))
         turn_wgt()
         for mb in range(M // P):
-            weigh_reach(0, mb)
-        picked0 = ring.tile([P, PACK, M], F32, name="picked", tag="wide", bufs=2, align_bytes=64)
-        collect(0, picked0, 0, M)
-        for i in range(1, PACK):
-            first_stage(1, i, whole, (S,))
-        for mb in range(M // P):
-            weigh_reach(1, mb)
-        for lo, hi in spans(whole):
-            quantise_z(0, picked0, lo, hi, nc.scalar.copy)
+            weigh_reach(mb)
 
-        tags = [("mm", 4)] * 4 + [("fw", 2)] * 2 + [("bk", 2)] * 2
-        banks = []
-        used = 0
-        for lo, hi in spans(LAST_CUTS):
-            per_bank = BANK // (hi - lo)
-            mine = []
-            for first in range(0, N // P, per_bank):
-                tag, bufs = tags[used]
-                used = used + 1
-                bank = psum.tile([P, per_bank, hi - lo], F32, name="scores", tag=tag, bufs=bufs)
-                for slot in range(per_bank):
-                    second_pass(0, bank, slot, first + slot, lo, hi, slot == 0, False)
-                mine.append((bank, first, per_bank))
-            banks.append(mine)
-
-        picked1 = ring.tile([P, PACK, M], F32, name="picked", tag="wide", bufs=2, align_bytes=64)
+        picked_tiles = [ring.tile([P, PACK * BANK], F32, name="picked%d" % b, tag="wide%d" % b, align_bytes=64) for b in range(2)]
         out_rows = out.rearrange("(t p) m -> p t m", p=P)
-        last = len(LAST_CUTS) - 1
-        for c, (lo, hi) in enumerate(spans(LAST_CUTS)):
-            collect(1, picked1, lo, hi)
-            quantise_z(1, picked1, lo, hi, nc.vector.tensor_copy if c == last else nc.scalar.copy)
-            staged = ring.tile([P, N // P, hi - lo], F32, name="staged", tag="h", bufs=3)
-            for bank, first, per_bank in banks[c]:
-                for slot in range(per_bank):
-                    second_pass(1, bank, slot, first + slot, lo, hi, False, slot == per_bank - 1)
+        cuts = spans(LAST_CUTS)
+        last = len(cuts) - 1
+        z_codes = {}
+
+        def prepare(c, b):
+            lo, hi = cuts[c]
+            k = 2 * c + b
+            picked = picked_tiles[b][:, 0 : PACK * (hi - lo)].rearrange("p (i m) -> p i m", i=PACK)
+            collect(b, picked, lo, hi)
+            z = ring.tile([P, PACK * (hi - lo)], BF16, name="z_%d" % k, tag="cut%d" % k, align_bytes=64)
+            z_codes[c, b] = ring.tile([P, hi - lo], U32, name="z_codes_%d" % k, tag="cut%d" % (k + 2), align_bytes=64)
+            copy = nc.vector.tensor_copy if (c, b) == (last, 1) else nc.scalar.copy
+            quantise_z(b, picked, lo, hi, copy, z[:], z_codes[c, b][:])
+
+        def finish(c):
+            lo, hi = cuts[c]
+            per_bank = BANK // (hi - lo)
+            staged = [take("h", h_tiles) for k in range(-(-(N // P) * (hi - lo) // S))]
+            per_tile = (N // P) // len(staged)
+            for first in range(0, N // P, per_bank):
+                bank = take_bank(per_bank, hi - lo)
+                for b in range(2):
+                    for slot in range(per_bank):
+                        start = b == 0 and slot == 0
+                        stop = b == 1 and slot == per_bank - 1
+                        second_pass(b, z_codes[c, b][:], bank, slot, first + slot, lo, hi, start, stop)
+                rows = staged[first // per_tile][:, 0 : per_tile * (hi - lo)].rearrange("p (t m) -> p t m", t=per_tile)
+                at = first % per_tile
                 if c == last:
                     nc.vector.tensor_tensor(
-                        staged[:, first : first + per_bank, :],
-                        bank[:],
+                        rows[:, at : at + per_bank, :],
+                        bank,
                         b2_t[:, first : first + per_bank].unsqueeze(2).to_broadcast([P, per_bank, hi - lo]),
                         ALU.add,
                     )
@@ -304,6 +329,14 @@ def tile_list_suction_grasp_scores_kernel(
                     for slot in range(per_bank):
                         nt = first + slot
                         nc.scalar.activation(
-                            staged[:, nt, :], bank[:, slot, :], ACT.Identity, bias=b2_t[:, nt : nt + 1]
+                            rows[:, at + slot, :], bank[:, slot, :], ACT.Identity, bias=b2_t[:, nt : nt + 1]
                         )
-            nc.sync.dma_start(out_rows[:, :, lo:hi], staged[:])
+                if at + per_bank == per_tile:
+                    nc.sync.dma_start(out_rows[:, first + per_bank - per_tile : first + per_bank, lo:hi], rows)
+
+        for c in range(len(cuts)):
+            prepare(c, 0)
+            if c > 0:
+                finish(c - 1)
+            prepare(c, 1)
+        finish(last)

@@ -24,6 +24,7 @@ PASS = P * PACK
 BANK = 512
 GROUP = 16
 RUNS = 8
+TURNED = 768
 FIRST_CUTS = (256, 256, 512)
 LAST_CUTS = (512, 256, 128, 128)
 
@@ -58,7 +59,6 @@ def tile_list_suction_grasp_scores_kernel(
         b2_t = keep.tile([P, N // P], F32, name="b2_t")
         ident = keep.tile([P, P], F32, name="ident")
 
-        v_planes = keep.tile([P, S], U8, name="v_planes", align_bytes=64)
         nc.vector.memset(tab_planes[:].bitcast(I32), 0)
         for q in range(4):
             nc.gpsimd.dma_start(
@@ -87,10 +87,11 @@ def tile_list_suction_grasp_scores_kernel(
         wgs_rows = wgs.rearrange("(p i) s -> p i s", i=PACK)
         wgs_t = {}
 
-        def load_wgs(i, pool, tag):
-            wgs_t[i] = pool.tile([P, S], F32, name="wgs_%d" % i, tag=tag)
-            for q in range(4):
-                nc.sync.dma_start(wgs_t[i][32 * q : 32 * (q + 1), :], wgs_rows[:, i, :])
+        def load_wgs(i, widths, tile):
+            wgs_t[i] = tile
+            for lo, hi in spans(widths):
+                for q in (0, 2, 1, 3):
+                    nc.sync.dma_start(wgs_t[i][32 * q : 32 * (q + 1), lo:hi], wgs_rows[:, i, lo:hi])
 
         wgt_t = keep.tile([P, M], F32, name="wgt_t")
 
@@ -103,20 +104,39 @@ def tile_list_suction_grasp_scores_kernel(
             tab.append(words)
         nc.sync.dma_start(list2[:], offs2)
         pages = {(0, 0): load_page(0, 0)}
-        load_wgs(0, keep, "wgs0")
+        load_wgs(0, (FIRST_CUTS[0], S - FIRST_CUTS[0]), keep.tile([P, S], F32, name="wgs_0"))
         pages[0, 1] = load_page(0, 1)
-        load_wgs(1, keep, "wgs1")
+        load_wgs(1, (S,), keep.tile([P, S], F32, name="wgs_1"))
+        pages[0, 2] = load_page(0, 2)
+
+        v_planes = keep.tile([P, S], U8, name="v_planes", align_bytes=64)
+        nc.vector.tensor_copy(v_planes[:], tab_planes[:].indirect(list1[:]))
+        v_words = [
+            keep.tile([P, S], U32, name="v_words_0", align_bytes=64),
+            ring.tile([P, S], U32, name="v_words_1", tag="planes", align_bytes=64),
+        ]
+        nc.vector.tensor_copy(v_words[0][:], tab[0][:].indirect(list1[:]))
+        for lo, hi in spans(FIRST_CUTS):
+            nc.vector.tensor_copy(v_words[1][:, lo:hi], tab[1][:].indirect(list1[:, lo // 16 : hi // 16]))
+        picked_tiles = [ring.tile([P, 2 * S], F32, name="picked%d" % b, tag="wide%d" % b, align_bytes=64) for b in range(2)]
+
+        load_wgs(2, (S,), picked_tiles[1][:, S:])
         for a in range(2):
             w1_raw[1, a] = load_w1(1, a)
-        pages[0, 2] = load_page(0, 2)
-        load_wgs(2, keep, "wgs2")
-        load_wgs(3, keep, "wgs3")
-        pages[0, 3] = load_page(0, 3)
-        for i in range(PACK):
-            pages[1, i] = load_page(1, i)
+        pages[0, PACK - 1] = load_page(0, PACK - 1)
+        load_wgs(PACK - 1, (S,), picked_tiles[0][:, S:])
+        pages[1, 0] = load_page(1, 0)
         nc.sync.dma_start(wgt_t[:], wgt)
         for g in range(RUNS):
-            nc.sync.dma_start(factor[:, g, :], reach_runs[g])
+            nc.sync.dma_start(factor[:, g, 0:BANK], reach_runs[g][:, :, 0:BANK])
+        pages[1, 1] = load_page(1, 1)
+        for g in range(RUNS):
+            nc.sync.dma_start(factor[:, g, BANK:TURNED], reach_runs[g][:, :, BANK:TURNED])
+        for i in range(2, PACK):
+            pages[1, i] = load_page(1, i)
+        for b in range(2):
+            rows = reach[b * PASS : (b + 1) * PASS, TURNED:M].rearrange("(p i) m -> p i m", i=PACK)
+            nc.sync.dma_start(factor[:, b * PACK : (b + 1) * PACK, TURNED:M], rows)
         nc.sync.dma_start(list3[:], offs3)
         nc.sync.dma_start(w4_codes[:].bitcast(I32), w4_words.rearrange("a p n -> p a n").bitcast(I32))
         for q in range(4):
@@ -166,17 +186,7 @@ def tile_list_suction_grasp_scores_kernel(
         for a in range(2):
             quantise_w1(0, a, nc.vector.tensor_copy)
 
-        nc.vector.tensor_copy(v_planes[:], tab_planes[:].indirect(list1[:]))
-        v_words = [
-            keep.tile([P, S], U32, name="v_words_0", align_bytes=64),
-            ring.tile([P, S], U32, name="v_words_1", tag="planes", align_bytes=64),
-        ]
-        nc.vector.tensor_copy(v_words[0][:], tab[0][:].indirect(list1[:]))
-        for lo, hi in spans(FIRST_CUTS):
-            nc.vector.tensor_copy(v_words[1][:, lo:hi], tab[1][:].indirect(list1[:, lo // 16 : hi // 16]))
-
-        def first_stage(b, i, matmul_cuts, tail_cuts):
-            h = take("h", h_tiles)
+        def first_stage(b, i, matmul_cuts, tail_cuts, h, result):
             rows = slice(i * P, (i + 1) * P)
             done = 0
             todo = spans(tail_cuts)
@@ -198,7 +208,7 @@ def tile_list_suction_grasp_scores_kernel(
                     done = done + 1
                     nc.scalar.activation(h[:, s0:s1], h[:, s0:s1], ACT.Square)
                     nc.scalar.activation(
-                        h[:, s0:s1],
+                        result[:, s0:s1],
                         h[:, s0:s1],
                         ACT.Identity,
                         bias=gain_t[:, b, i : i + 1],
@@ -206,7 +216,7 @@ def tile_list_suction_grasp_scores_kernel(
                     )
                     weights = wgs_t[i][:, s0:s1]
                     nc.vector.tensor_tensor(
-                        pages[b, i][:].indirect(list2[:, s0 // 16 : s1 // 16]), h[:, s0:s1], weights, ALU.mult
+                        pages[b, i][:].indirect(list2[:, s0 // 16 : s1 // 16]), result[:, s0:s1], weights, ALU.mult
                     )
 
         wgt_cols = keep.tile([P, M // P, P // GROUP], F32, name="wgt_cols")
@@ -274,21 +284,30 @@ def tile_list_suction_grasp_scores_kernel(
             )
 
         whole = (BANK, BANK)
-        first_stage(0, 0, FIRST_CUTS, FIRST_CUTS)
+        first_stage(0, 0, FIRST_CUTS, FIRST_CUTS, h_tiles[0], h_tiles[0])
         for i in range(1, PACK - 1):
-            first_stage(0, i, whole, (S,))
+            first_stage(0, i, whole, (S,), h_tiles[i], h_tiles[i])
         for a in range(2):
             quantise_w1(1, a, nc.scalar.copy)
-        for a in (1, 0):
-            h_tiles.append(ring.tile([P, S], F32, name="h_late%d" % a, tag="raw%d" % a))
-        first_stage(0, PACK - 1, whole, (S,))
-        for i in range(PACK):
-            first_stage(1, i, whole, (S,))
+        late = [ring.tile([P, S], F32, name="h_late%d" % a, tag="raw%d" % a) for a in range(2)]
+        first_stage(0, PACK - 1, whole, (S,), h_tiles[0], late[1])
+        first_stage(1, 0, whole, whole, late[0], late[0])
+        first_stage(1, 1, whole, (S,), h_tiles[1], h_tiles[1])
         turn_wgt()
-        for mb in range(M // P):
+        weigh_reach(0)
+        first_stage(1, 2, whole, (S,), picked_tiles[1][:, 0:S], picked_tiles[1][:, 0:S])
+        weigh_reach(1)
+        first_stage(1, 3, whole, (S,), picked_tiles[0][:, 0:S], picked_tiles[0][:, 0:S])
+        for mb in range(2, TURNED // P):
             weigh_reach(mb)
+        nc.vector.tensor_tensor(
+            factor[:, :, TURNED:M],
+            factor[:, :, TURNED:M],
+            wgt_t[:, TURNED:M].unsqueeze(1).to_broadcast([P, RUNS, M - TURNED]),
+            ALU.mult,
+        )
+        h_tiles.extend(late)
 
-        picked_tiles = [ring.tile([P, PACK * BANK], F32, name="picked%d" % b, tag="wide%d" % b, align_bytes=64) for b in range(2)]
         out_rows = out.rearrange("(t p) m -> p t m", p=P)
         cuts = spans(LAST_CUTS)
         last = len(cuts) - 1

@@ -24,7 +24,7 @@ PASS = P * PACK
 BANK = 512
 GROUP = 16
 RUNS = 8
-TURNED = 768
+TURNED = 896
 FIRST_CUTS = (256, 256, 512)
 LAST_CUTS = (512, 256, 128, 128)
 
@@ -51,7 +51,7 @@ def tile_list_suction_grasp_scores_kernel(
         list2 = keep.tile([P, S // 16], U16, name="list2")
         list3 = keep.tile([P, M // 16], U16, name="list3")
 
-        tab_planes = ring.tile([P, T], U8, name="tab_planes", tag="planes", align_bytes=64)
+        tab_planes = keep.tile([P, T], U8, name="tab_planes", align_bytes=64)
         w4_planes = keep.tile([P, 2, N], U8, name="w4_planes", align_bytes=64)
         w4_codes = keep.tile([P, 2, 2 * N], U8, name="w4_codes", align_bytes=64)
         b1_t = keep.tile([P, 2, PACK], F32, name="b1_t")
@@ -60,13 +60,7 @@ def tile_list_suction_grasp_scores_kernel(
         ident = keep.tile([P, P], F32, name="ident")
 
         nc.vector.memset(tab_planes[:].bitcast(I32), 0)
-        for q in range(4):
-            nc.gpsimd.dma_start(
-                tab_planes[32 * q : 32 * q + 8, :].bitcast(I32), tab_scales[:, 4 * q : 4 * q + 4, :].bitcast(I32)
-            )
         nc.vector.memset(w4_planes[:].rearrange("p a n -> p (a n)").bitcast(I32), 0)
-        nc.scalar.dma_start(b1_t[:], b1.rearrange("(b p i) -> p b i", b=2, i=PACK))
-        nc.scalar.dma_start(gain_t[:], gain.rearrange("(b p i) -> p b i", b=2, i=PACK))
         make_identity(nc, ident[:])
 
         def load_w1(b, a):
@@ -96,7 +90,14 @@ def tile_list_suction_grasp_scores_kernel(
         wgt_t = keep.tile([P, M], F32, name="wgt_t")
 
         nc.sync.dma_start(list1[:], offs)
-        w1_raw = {(0, a): load_w1(0, a) for a in range(2)}
+        nc.sync.dma_start(gain_t[:], gain.rearrange("(b p i) -> p b i", b=2, i=PACK))
+        nc.sync.dma_start(b1_t[:], b1.rearrange("(b p i) -> p b i", b=2, i=PACK))
+        w1_raw = {(0, 0): load_w1(0, 0)}
+        w1_raw[0, 1] = load_w1(0, 1)
+        for q in range(4):
+            nc.sync.dma_start(
+                tab_planes[32 * q : 32 * q + 8, :].bitcast(I32), tab_scales[:, 4 * q : 4 * q + 4, :].bitcast(I32)
+            )
         tab = []
         for a in range(2):
             words = ring.tile([P, T], U32, name="tab_words_t", tag="wide%d" % a, align_bytes=64)
@@ -110,11 +111,8 @@ def tile_list_suction_grasp_scores_kernel(
         pages[0, 2] = load_page(0, 2)
 
         v_planes = keep.tile([P, S], U8, name="v_planes", align_bytes=64)
+        v_words = [keep.tile([P, S], U32, name="v_words_%d" % a, align_bytes=64) for a in range(2)]
         nc.vector.tensor_copy(v_planes[:], tab_planes[:].indirect(list1[:]))
-        v_words = [
-            keep.tile([P, S], U32, name="v_words_0", align_bytes=64),
-            ring.tile([P, S], U32, name="v_words_1", tag="planes", align_bytes=64),
-        ]
         nc.vector.tensor_copy(v_words[0][:], tab[0][:].indirect(list1[:]))
         for lo, hi in spans(FIRST_CUTS):
             nc.vector.tensor_copy(v_words[1][:, lo:hi], tab[1][:].indirect(list1[:, lo // 16 : hi // 16]))
@@ -183,8 +181,8 @@ def tile_list_suction_grasp_scores_kernel(
             w1_codes[b, a] = codes
             w1_planes[b, a] = plane
 
-        for a in range(2):
-            quantise_w1(0, a, nc.vector.tensor_copy)
+        quantise_w1(0, 0, nc.scalar.copy)
+        quantise_w1(0, 1, nc.vector.tensor_copy)
 
         def first_stage(b, i, matmul_cuts, tail_cuts, h, result):
             rows = slice(i * P, (i + 1) * P)

import math
from contextlib import ExitStack

import concourse.mybir as mybir
from concourse.masks import make_identity

K, T, S, T2, M, H, N = 1024, 4096, 1024, 2048, 1024, 1024, 512
FLOPS = 2 * K * H * S + 2 * H * N * M

F32 = mybir.dt.float32
BF16 = mybir.dt.bfloat16
I32 = mybir.dt.int32
U32 = mybir.dt.uint32
U16 = mybir.dt.uint16
U8 = mybir.dt.uint8
FP8X4 = mybir.dt.float8_e4m3fn_x4
FP4X4 = mybir.dt.float4_e2m1fn_x4
ALU = mybir.AluOpType
ACT = mybir.ActivationFunctionType

P = 128
PACK = 4
PASS = P * PACK
BANK = 512
GROUP = 16
RUNS = 8
TURNED = 896
FIRST_CUTS = (256, 256, 512)
LAST_CUTS = (512, 256, 128, 128)


def spans(widths):
    start = 0
    result = []
    for width in widths:
        result.append((start, start + width))
        start = start + width
    return result


def tile_list_suction_grasp_scores_kernel(
    tc, tab_words, tab_scales, offs, w1, b1, gain, page0, wgs, offs2, wgt, offs3, reach, w4_words, w4_scales, b2, out
):
    nc = tc.nc
    with ExitStack() as ctx:
        keep = ctx.enter_context(tc.tile_pool(name="keep", bufs=1))
        ring = ctx.enter_context(tc.tile_pool(name="ring", bufs=1))
        psum = ctx.enter_context(tc.psum_pool(name="psum", bufs=1))

        list1 = keep.tile([P, S // 16], U16, name="list1")
        list2 = keep.tile([P, S // 16], U16, name="list2")
        list3 = keep.tile([P, M // 16], U16, name="list3")

        tab_planes = keep.tile([P, T], U8, name="tab_planes", align_bytes=64)
        w4_planes = keep.tile([P, 2, N], U8, name="w4_planes", align_bytes=64)
        w4_codes = keep.tile([P, 2, 2 * N], U8, name="w4_codes", align_bytes=64)
        b1_t = keep.tile([P, 2, PACK], F32, name="b1_t")
        gain_t = keep.tile([P, 2, PACK], F32, name="gain_t")
        b2_t = keep.tile([P, N // P], F32, name="b2_t")
        ident = keep.tile([P, P], F32, name="ident")

        nc.vector.memset(tab_planes[:].bitcast(I32), 0)
        nc.vector.memset(w4_planes[:].rearrange("p a n -> p (a n)").bitcast(I32), 0)
        make_identity(nc, ident[:])

        def load_w1(b, a):
            raw = ring.tile([P, PACK, PASS], F32, name="w1_raw", tag="raw%d" % a)
            rows = w1[a * PASS : (a + 1) * PASS, b * PASS : (b + 1) * PASS]
            nc.sync.dma_start(raw[:], rows.rearrange("(p j) c -> p j c", j=PACK))
            return raw

        def load_page(b, i):
            page = keep.tile([P, T2], F32, name="page_%d_%d" % (b, i))
            rows = page0[b * PASS : (b + 1) * PASS, :].rearrange("(p i) c -> p i c", i=PACK)
            nc.sync.dma_start(page[:], rows[:, i, :])
            return page

        factor = keep.tile([P, RUNS, M], F32, name="factor")
        reach_runs = reach.rearrange("(b g r) m -> g r b m", b=2, g=RUNS)

        wgs_rows = wgs.rearrange("(p i) s -> p i s", i=PACK)
        wgs_t = {}

        def load_wgs(i, widths, tile):
            wgs_t[i] = tile
            for lo, hi in spans(widths):
                for q in (0, 2, 1, 3):
                    nc.sync.dma_start(wgs_t[i][32 * q : 32 * (q + 1), lo:hi], wgs_rows[:, i, lo:hi])

        wgt_t = keep.tile([P, M], F32, name="wgt_t")

        nc.sync.dma_start(list1[:], offs)
        nc.sync.dma_start(gain_t[:], gain.rearrange("(b p i) -> p b i", b=2, i=PACK))
        nc.sync.dma_start(b1_t[:], b1.rearrange("(b p i) -> p b i", b=2, i=PACK))
        w1_raw = {(0, 0): load_w1(0, 0)}
        w1_raw[0, 1] = load_w1(0, 1)
        for q in range(4):
            nc.sync.dma_start(
                tab_planes[32 * q : 32 * q + 8, :].bitcast(I32), tab_scales[:, 4 * q : 4 * q + 4, :].bitcast(I32)
            )
        tab = []
        for a in range(2):
            words = ring.tile([P, T], U32, name="tab_words_t", tag="wide%d" % a, align_bytes=64)
            nc.sync.dma_start(words[:].bitcast(I32), tab_words[a].rearrange("p t i -> p (t i)").bitcast(I32))
            tab.append(words)
        nc.sync.dma_start(list2[:], offs2)
        pages = {(0, 0): load_page(0, 0)}
        load_wgs(0, (FIRST_CUTS[0], S - FIRST_CUTS[0]), keep.tile([P, S], F32, name="wgs_0"))
        pages[0, 1] = load_page(0, 1)
        load_wgs(1, (S,), keep.tile([P, S], F32, name="wgs_1"))
        pages[0, 2] = load_page(0, 2)

        v_planes = keep.tile([P, S], U8, name="v_planes", align_bytes=64)
        v_words = [keep.tile([P, S], U32, name="v_words_%d" % a, align_bytes=64) for a in range(2)]
        nc.vector.tensor_copy(v_planes[:], tab_planes[:].indirect(list1[:]))
        nc.vector.tensor_copy(v_words[0][:], tab[0][:].indirect(list1[:]))
        for lo, hi in spans(FIRST_CUTS):
            nc.vector.tensor_copy(v_words[1][:, lo:hi], tab[1][:].indirect(list1[:, lo // 16 : hi // 16]))
        picked_tiles = [ring.tile([P, 2 * S], F32, name="picked%d" % b, tag="wide%d" % b, align_bytes=64) for b in range(2)]

        load_wgs(2, (S,), picked_tiles[1][:, S:])
        for a in range(2):
            w1_raw[1, a] = load_w1(1, a)
        pages[0, PACK - 1] = load_page(0, PACK - 1)
        load_wgs(PACK - 1, (S,), picked_tiles[0][:, S:])
        pages[1, 0] = load_page(1, 0)
        nc.sync.dma_start(wgt_t[:], wgt)
        for g in range(RUNS):
            nc.sync.dma_start(factor[:, g, 0:BANK], reach_runs[g][:, :, 0:BANK])
        pages[1, 1] = load_page(1, 1)
        for g in range(RUNS):
            nc.sync.dma_start(factor[:, g, BANK:TURNED], reach_runs[g][:, :, BANK:TURNED])
        for i in range(2, PACK):
            pages[1, i] = load_page(1, i)
        for b in range(2):
            rows = reach[b * PASS : (b + 1) * PASS, TURNED:M].rearrange("(p i) m -> p i m", i=PACK)
            nc.sync.dma_start(factor[:, b * PACK : (b + 1) * PACK, TURNED:M], rows)
        nc.sync.dma_start(list3[:], offs3)
        nc.sync.dma_start(w4_codes[:].bitcast(I32), w4_words.rearrange("a p n -> p a n").bitcast(I32))
        for q in range(4):
            nc.sync.dma_start(
                w4_planes[32 * q : 32 * q + 4, :, :].bitcast(I32),
                w4_scales[:, 4 * q : 4 * q + 4, :].rearrange("a r n -> r a n").bitcast(I32),
            )
        with nc.allow_non_contiguous_dma(reason="one bias value a partition"):
            nc.sync.dma_start(b2_t[:], b2.rearrange("(t p) -> p t", p=P))

        psum_banks = [psum.tile([P, BANK], F32, name="bank%d" % k) for k in range(8)]
        h_tiles = [keep.tile([P, S], F32, name="h%d" % k) for k in range(3)]
        bf_tiles = [keep.tile([P, 2048], BF16, name="bf%d" % k, align_bytes=64) for k in range(2)]
        scaled_tiles = [keep.tile([P, 2, PACK, P], F32, name="scaled%d" % k) for k in range(2)]
        turns = {"bank": 0, "h": 0, "bf": 0, "scaled": 0}

        def take(kind, tiles):
            tile = tiles[turns[kind] % len(tiles)]
            turns[kind] = turns[kind] + 1
            return tile

        def take_bank(count, width):
            return take("bank", psum_banks)[:, 0 : count * width].rearrange("p (u w) -> p u w", u=count)

        half_bias = keep.tile([P, 2, PACK], F32, name="half_bias")
        minus_two_gain = keep.tile([P, 2, PACK], F32, name="minus_two_gain")
        nc.gpsimd.tensor_scalar(half_bias[:], b1_t[:], 0.5, -math.pi / 4, ALU.mult, ALU.add)
        nc.scalar.activation(minus_two_gain[:], gain_t[:], ACT.Copy, scale=-2.0)

        w1_codes = {}
        w1_planes = {}

        def quantise_w1(b, a, copy):
            grouped = take("bf", bf_tiles)
            copy(
                grouped[:].rearrange("p (t m j) -> p m j t", t=PACK, j=PACK),
                w1_raw[b, a][:].rearrange("p j (m t) -> p m j t", t=PACK),
            )
            codes = keep.tile([P, PASS], U32, name="w1_codes_%d_%d" % (b, a), align_bytes=64)
            plane = keep.tile([P, PASS], U8, name="w1_plane_%d_%d" % (b, a), align_bytes=64)
            nc.vector.quantize_mx(
                out=codes[:].bitcast(FP8X4), scales=plane[:], in_=grouped[:]
            )
            w1_codes[b, a] = codes
            w1_planes[b, a] = plane

        quantise_w1(0, 0, nc.scalar.copy)
        quantise_w1(0, 1, nc.vector.tensor_copy)

        def first_stage(b, i, matmul_cuts, tail_cuts, h, result):
            rows = slice(i * P, (i + 1) * P)
            done = 0
            todo = spans(tail_cuts)
            for lo, hi in spans(matmul_cuts):
                acc = take("bank", psum_banks)[:, 0 : hi - lo]
                for a in range(2):
                    nc.tensor.matmul_mx(
                        out=acc,
                        lhsT=w1_codes[b, a][:, rows].bitcast(FP8X4),
                        lhsT_scale=w1_planes[b, a][:, rows],
                        rhs=v_words[a][:, lo:hi].bitcast(FP8X4),
                        rhs_scale=v_planes[PACK * a :, lo:hi],
                        start=(a == 0),
                        stop=(a == 1),
                    )
                nc.scalar.activation(h[:, lo:hi], acc, ACT.Sin, bias=half_bias[:, b, i : i + 1], scale=0.5)
                if hi == todo[done][1]:
                    s0, s1 = todo[done]
                    done = done + 1
                    nc.scalar.activation(h[:, s0:s1], h[:, s0:s1], ACT.Square)
                    nc.scalar.activation(
                        result[:, s0:s1],
                        h[:, s0:s1],
                        ACT.Identity,
                        bias=gain_t[:, b, i : i + 1],
                        scale=minus_two_gain[:, b, i : i + 1],
                    )
                    weights = wgs_t[i][:, s0:s1]
                    nc.vector.tensor_tensor(
                        pages[b, i][:].indirect(list2[:, s0 // 16 : s1 // 16]), result[:, s0:s1], weights, ALU.mult
                    )

        wgt_cols = keep.tile([P, M // P, P // GROUP], F32, name="wgt_cols")

        def turn_wgt():
            for half in range(2):
                bank = take_bank(PACK, P)
                for u in range(PACK):
                    mb = half * PACK + u
                    nc.tensor.transpose(bank[:, u, :], wgt_t[:, mb * P : (mb + 1) * P], ident[:])
                nc.scalar.copy(wgt_cols[:, half * PACK : (half + 1) * PACK, :], bank[:, :, 0:P:GROUP])

        def weigh_reach(mb):
            cols = slice(mb * P, (mb + 1) * P)
            scaled = take("scaled", scaled_tiles)
            for half in range(2):
                turned = take_bank(PACK, P)
                for u in range(PACK):
                    nc.tensor.transpose(turned[:, u, :], factor[:, half * PACK + u, cols], ident[:])
                for u in range(PACK):
                    g = half * PACK + u
                    nc.scalar.activation(
                        scaled[:, :, :, g * GROUP : (g + 1) * GROUP],
                        turned[:, u, :].rearrange("m (p i b) -> m b i p", i=PACK, b=2),
                        ACT.Copy,
                        scale=wgt_cols[:, mb, g : g + 1],
                    )
            for b in range(2):
                back = take_bank(PACK, P)
                for i in range(PACK):
                    nc.tensor.transpose(back[:, i, :], scaled[:, b, i, :], ident[:])
                nc.scalar.copy(factor[:, b * PACK : (b + 1) * PACK, cols], back)

        z_planes = [keep.tile([P, M], U8, name="z_planes_%d" % b, align_bytes=64) for b in range(2)]

        def collect(b, picked, lo, hi):
            for i in range(PACK):
                nc.vector.tensor_tensor(
                    picked[:, i, :],
                    pages[b, i][:].indirect(list3[:, lo // 16 : hi // 16]),
                    factor[:, b * PACK + i, lo:hi],
                    ALU.mult,
                )

        def quantise_z(b, picked, lo, hi, copy, z, codes):
            copy(
                z.rearrange("p (c k i) -> p c i k", k=4, i=PACK),
                picked.rearrange("p i (c k) -> p c i k", k=4),
            )
            nc.vector.quantize_mx(
                out=codes.bitcast(FP8X4),
                scales=z_planes[b][:, lo:hi],
                in_=z,
            )

        def second_pass(b, codes, bank, slot, nt, lo, hi, start, stop):
            nc.tensor.matmul_mx(
                out=bank[:, slot, :],
                lhsT=w4_codes[:, b, 2 * nt * P : 2 * (nt + 1) * P].bitcast(FP4X4),
                lhsT_scale=w4_planes[:, b, nt * P : (nt + 1) * P],
                rhs=codes.bitcast(FP8X4),
                rhs_scale=z_planes[b][:, lo:hi],
                start=start,
                stop=stop,
            )

        whole = (BANK, BANK)
        first_stage(0, 0, FIRST_CUTS, FIRST_CUTS, h_tiles[0], h_tiles[0])
        for i in range(1, PACK - 1):
            first_stage(0, i, whole, (S,), h_tiles[i], h_tiles[i])
        for a in range(2):
            quantise_w1(1, a, nc.scalar.copy)
        late = [ring.tile([P, S], F32, name="h_late%d" % a, tag="raw%d" % a) for a in range(2)]
        first_stage(0, PACK - 1, whole, (S,), h_tiles[0], late[1])
        first_stage(1, 0, whole, whole, late[0], late[0])
        first_stage(1, 1, whole, (S,), h_tiles[1], h_tiles[1])
        turn_wgt()
        weigh_reach(0)
        first_stage(1, 2, whole, (S,), picked_tiles[1][:, 0:S], picked_tiles[1][:, 0:S])
        weigh_reach(1)
        first_stage(1, 3, whole, (S,), picked_tiles[0][:, 0:S], picked_tiles[0][:, 0:S])
        for mb in range(2, TURNED // P):
            weigh_reach(mb)
        nc.vector.tensor_tensor(
            factor[:, :, TURNED:M],
            factor[:, :, TURNED:M],
            wgt_t[:, TURNED:M].unsqueeze(1).to_broadcast([P, RUNS, M - TURNED]),
            ALU.mult,
        )
        h_tiles.extend(late)

        out_rows = out.rearrange("(t p) m -> p t m", p=P)
        cuts = spans(LAST_CUTS)
        last = len(cuts) - 1
        z_codes = {}

        def prepare(c, b):
            lo, hi = cuts[c]
            k = 2 * c + b
            picked = picked_tiles[b][:, 0 : PACK * (hi - lo)].rearrange("p (i m) -> p i m", i=PACK)
            collect(b, picked, lo, hi)
            z = ring.tile([P, PACK * (hi - lo)], BF16, name="z_%d" % k, tag="cut%d" % k, align_bytes=64)
            z_codes[c, b] = ring.tile([P, hi - lo], U32, name="z_codes_%d" % k, tag="cut%d" % (k + 2), align_bytes=64)
            copy = nc.vector.tensor_copy if (c, b) == (last, 1) else nc.scalar.copy
            quantise_z(b, picked, lo, hi, copy, z[:], z_codes[c, b][:])

        def finish(c):
            lo, hi = cuts[c]
            per_bank = BANK // (hi - lo)
            staged = [take("h", h_tiles) for k in range(-(-(N // P) * (hi - lo) // S))]
            per_tile = (N // P) // len(staged)
            for first in range(0, N // P, per_bank):
                bank = take_bank(per_bank, hi - lo)
                for b in range(2):
                    for slot in range(per_bank):
                        start = b == 0 and slot == 0
                        stop = b == 1 and slot == per_bank - 1
                        second_pass(b, z_codes[c, b][:], bank, slot, first + slot, lo, hi, start, stop)
                rows = staged[first // per_tile][:, 0 : per_tile * (hi - lo)].rearrange("p (t m) -> p t m", t=per_tile)
                at = first % per_tile
                if c == last:
                    nc.vector.tensor_tensor(
                        rows[:, at : at + per_bank, :],
                        bank,
                        b2_t[:, first : first + per_bank].unsqueeze(2).to_broadcast([P, per_bank, hi - lo]),
                        ALU.add,
                    )
                else:
                    for slot in range(per_bank):
                        nt = first + slot
                        nc.scalar.activation(
                            rows[:, at + slot, :], bank[:, slot, :], ACT.Identity, bias=b2_t[:, nt : nt + 1]
                        )
                if at + per_bank == per_tile:
                    nc.sync.dma_start(out_rows[:, first + per_bank - per_tile : first + per_bank, lo:hi], rows)

        for c in range(len(cuts)):
            prepare(c, 0)
            if c > 0:
                finish(c - 1)
            prepare(c, 1)
        finish(last)
